import numpy as np, ml_dtypes
CORES = [16,17,18,19,32,33,34,35]
N = 8
BF = ml_dtypes.bfloat16
def f(rng, *shape):
    return (rng.standard_normal(shape, dtype=np.float32) * np.exp2(rng.integers(-2, 3, shape[:-1] + (1,)))).astype(BF)
def wide(rng, *shape):
    v = f(rng, *shape).astype(np.float32); k = shape[:-2] + (1, shape[-1])
    return (v * np.exp2(rng.integers(-6, 7, k)) * (rng.random(k) > 0.0625)).astype(BF)
D, H, B, R = 64, 8, 1, 3
STEP = 2.0 ** -12
def pack(cs):
    a = np.asarray(cs).reshape(N, B, 8, 2).transpose(0, 2, 1, 3).reshape(N, 8, 1, 2 * B)
    return np.ascontiguousarray(np.repeat(a, 16, axis=2).reshape(N, 128, 2 * B)).astype(np.int32)
def stripes(v):
    return np.ascontiguousarray(v.reshape(16, N, H * D).transpose(1, 0, 2))
def pictures(v):
    return np.ascontiguousarray(v.transpose(1, 0, 2)).reshape(16, D * D)
def setup_inputs(rng):
    A = 8 * B * N; th = 2 * np.pi * (rng.permutation(A) + 0.8 * rng.random(A)) / A
    fac = np.exp2(rng.permutation(np.repeat(np.array([-4, -2, 0, 1]), 4))).astype(np.float32)
    x = np.abs(f(rng, N, 16, H * D).astype(np.float32))
    mu = (rng.random((N, 16, H * D)) * 0.06 * (rng.random((N, 16, H * D)) > 0.2)).astype(np.float32)
    counts = np.abs(f(rng, N, 128, B * D).astype(np.float32)) * np.float32(64) * np.tile(fac, 8)[:, None]
    return {"x": x, "mu": mu, "counts": counts, "ang": pack(np.stack([np.rint(256 * np.cos(th)), np.rint(256 * np.sin(th))], -1))}
def setup_inputs_axes(rng):
    d = setup_inputs(rng); A = 8 * B * N
    t = np.array([[256, 0], [0, 256], [-256, 0], [0, -256], [181, 181], [-181, 181], [181, -181], [-181, -181]])
    d["ang"] = pack(t[rng.permutation(np.arange(A) % 8)]); return d
def setup_inputs_pairs(rng):
    d = setup_inputs(rng); A = 8 * B * N; cs = rng.integers(-256, 257, (A, 2))
    cs[rng.permutation(A)[:8]] = np.array([[0, 0], [256, 256], [-256, 256], [256, -256], [-256, -256], [1, 0], [0, -1], [5, -9]])
    d["ang"] = pack(cs); return d
def setup_inputs_edges(rng):
    d = setup_inputs(rng); m = np.zeros((D, D), np.float32); m[[0, -1]] = 1; m[:, [0, -1]] = 1
    d["x"] = stripes((4 * pictures(d["x"]) * m.reshape(-1)).astype(np.float32)); return d
def setup_inputs_clear(rng):
    d = setup_inputs(rng); o = rng.permutation(16); mu = d["mu"].copy(); mu[:, o[:5]] = 0
    mu[:, o[5:9]] = np.minimum(rng.random((N, 4, H * D)) + 0.5, 1).astype(np.float32); d["mu"] = mu
    c = d["counts"].reshape(N, 8, 16, B * D).copy(); c[:, :, o[3:7]] = 0; d["counts"] = c.reshape(N, 128, B * D); return d
def setup_inputs_spread(rng):
    d = setup_inputs(rng); d["x"] = wide(rng, N, 16, H * D).astype(np.float32)
    d["counts"] = wide(rng, N, 128, B * D).astype(np.float32) * np.float32(64); return d
def check_inputs(d):
    bad = [k for k in ("x", "counts") if not np.isfinite(d[k]).all()]
    m = d["mu"]; a = d["ang"]; g = a.reshape(N, 8, 16, 2 * B)
    if not (np.isfinite(m).all() and (m >= 0).all() and (m <= 1).all()): bad.append("mu between 0 and 1")
    if ((a < -256) | (a > 256)).any(): bad.append("ang between -256 and 256")
    if (g != g[:, :, :1]).any(): bad.append("ang alike in a group")
    return bad
def cells(c, sn):
    a = 2 * np.arange(D)[None, None, :] - (D - 1); b = 2 * np.arange(D)[None, :, None] - (D - 1)
    c = c[:, None, None]; sn = sn[:, None, None]
    col = (c * a - sn * b + 256 * D) >> 9; row = (sn * a + c * b + 256 * D) >> 9
    ok = (col >= 0) & (col < D) & (row >= 0) & (row < D)
    return np.where(ok, D * row + col, D * D).reshape(-1, D * D)
def zero_end(v):
    return np.concatenate([v, np.zeros((16, 1))], 1)
def reference(x, mu, counts, ang):
    cs = ang.reshape(N, 8, 16, B, 2)[:, :, 0].transpose(0, 2, 1, 3).reshape(-1, 2).astype(np.int64)
    cnt = counts.reshape(N, 8, 16, B, D).transpose(0, 3, 1, 2, 4).reshape(-1, 16, D).astype(np.float64)
    there = cells(cs[:, 0], cs[:, 1]); back = cells(cs[:, 0], -cs[:, 1]); A = len(cs)
    M = zero_end(pictures(mu).astype(np.float64)); X = pictures(x).astype(np.float64)
    W = [np.exp(-np.add.accumulate(np.take(M, there[a], axis=1).reshape(16, D, D), axis=1)) for a in range(A)]
    for k in range(R):
        Z = zero_end(X); G = np.zeros((16, D * D))
        for a in range(A):
            e = cnt[a] - np.add.reduce(W[a] * np.take(Z, there[a], axis=1).reshape(16, D, D), axis=1)
            G += np.take(zero_end((W[a] * e[:, None, :]).reshape(16, D * D)), back[a], axis=1)
        X = np.maximum(X + STEP * G, 0)
    return {"y": stripes(X).astype(np.float32)}

@@ -1,0 +1,338 @@
+from concourse.bass import DstId, RemoteDMATransfer
+from concourse.mybir import AluOpType as A, ActivationFunctionType as AF
+
+R = 3
+STEP = 2.0 ** -12
+KQ = 0.00012918686694904754
+QUAD = [(1.1219518404595346, 18.754011438386996), (-4.267052247540635, 2.746736091488364),
+        (-1.8906565018022652, 14.883958171039492)]
+SCRATCH = {}
+for _n, _w in (("mc", 64), ("dx", 128), ("pdx", 128), ("angf", 4), ("cnt", 64), ("sq", 192), ("rq", 320), ("rep", 1024),
+               ("eye", 128), ("ssum", 16), ("ssel", 16), ("fm", 1), ("a64", 64), ("b4i", 4), ("b4", 4), ("kc", 4), ("kr", 4),
+               ("pen", 256), ("raw", 256), ("raw2", 256), ("D", 4104), ("X", 4104), ("W", 4104), ("f", 4104), ("z0", 4096),
+               ("xg", 4096), ("st", 4096), ("wb", 4096), ("pr", 4096), ("eg", 3072), ("u", 64), ("e", 64), ("snd", 1536),
+               ("lnd", 1152), ("t1", 64), ("t2", 64), ("pt", 384), ("xs", 384), ("rp", 1024), ("ysb", 512)):
+    SCRATCH[_n] = ("sbuf", [128, _w], "float32")
+for _n, _w in (("angi", 2), ("ipz", 16), ("ipz2", 16), ("ip", 1), ("ip2", 1), ("vc", 256), ("vr", 256), ("col", 256),
+               ("row", 256), ("tp", 256)):
+    SCRATCH[_n] = ("sbuf", [128, _w], "int32")
+for _n in ("fl", "tl"):
+    SCRATCH[_n] = ("sbuf", [128, 256], "uint16")
+for _n in range(8):
+    SCRATCH["bank%d" % _n] = ("psum", [128, 512], "float32")
+SEMAPHORES = (["v", "s", "p", "q", "ldm", "ldx", "lda", "ldc", "yo", "cx", "lr"]
+              + ["pd0", "pd1", "pw0", "pw1", "ld0", "ld1", "lw0", "lw1"]
+              + ["%s_%d_%d" % (n, k, s) for n in ("rs", "xc", "pu", "lp") for k in range(R) for s in range(2)])
+
+
+def ts(out, i, s1, o0, s2=None, o1=None):
+    if o1 is None:
+        return lambda e: e.tensor_scalar(out, i, s1, None, o0)
+    return lambda e: e.tensor_scalar(out, i, s1, s2, o0, o1)
+
+
+def tt(out, a, b, o):
+    return lambda e: e.tensor_tensor(out, a, b, o)
+
+
+def cp(out, i):
+    return lambda e: e.tensor_copy(out, i)
+
+
+def act(out, i, fn=AF.Copy, scale=1.0):
+    return lambda e: e.activation(out, i, fn, scale=scale)
+
+
+def mm(out, l, r, a, z):
+    return lambda e: e.matmul(out, l, r, a, z)
+
+
+def ms(ap, c):
+    return lambda e: e.memset(ap, c)
+
+
+def scan(out, d0, d1):
+    return lambda e: e.tensor_tensor_scan(out, d0, d1, 0.0, A.mult, A.add)
+
+
+def rank_program(g, core, T, topo):
+    rank = T.rank_of(core)
+    if rank is None:
+        return
+    chips = []
+    for c in T.cores:
+        if topo.chip(c) not in chips:
+            chips.append(topo.chip(c))
+    members = [[r for r, c in enumerate(T.cores) if topo.chip(c) == ch] for ch in chips]
+    ci = chips.index(topo.chip(core))
+    mine = members[ci]
+    me = mine.index(rank)
+    NQ = len(mine)
+    partner = members[1 - ci][me]
+    peers = [mine[(me + k) % NQ] for k in range(1, NQ)]
+    on_mask = topo.mask(core, T.cores[peers[0]])
+    ne_on = len(topo.engines(core, T.cores[peers[0]]))
+    ne_off = len(topo.engines(core, T.cores[partner]))
+    npush = ne_on * (NQ - 1)
+
+    ENG = {"v": g.vector, "s": g.scalar, "p": g.tensor, "q": g, "y": g.sync}
+    cnt, known, touch, sent, hist = {}, {}, {}, {}, {}
+
+    def wait(eng, sem, val):
+        if known.get((eng, sem), 0) < val:
+            ENG[eng].wait_ge(T.sem[sem], val)
+            known[(eng, sem)] = val
+
+    def waits(eng, deps):
+        for d in deps:
+            if d is not None:
+                wait(eng, d[0], d[1])
+
+    def op(eng, fn, deps=(), bank=None):
+        waits(eng, deps)
+        use = touch.setdefault(bank, {}) if bank is not None else {}
+        for (o, n) in use.items():
+            if o != eng:
+                wait(eng, o, n)
+        fn(ENG[eng]).then_inc(T.sem[eng], 1)
+        cnt[eng] = cnt.get(eng, 0) + 1
+        use[eng] = cnt[eng]
+        return (eng, cnt[eng])
+
+    def load(eng, out, in_, sem):
+        ENG[eng].dma_start(out, in_).then_inc(T.sem[sem], 16)
+        return (sem, 16)
+
+    def send(dst, out, in_, rsem, deps):
+        waits("q", deps)
+        c = T.cores[dst]
+        rid, pid, _ = topo.addr(c)
+        g.remote_dma(out, in_, T.sem[rsem], T.sem.lr, pid, rid, topo.mask(core, c))
+        sent["lr"] = sent.get("lr", 0) + len(topo.engines(core, c))
+
+    def push(ap, rsem, lsem, deps):
+        waits("q", deps)
+        ids = [DstId(rid=topo.addr(T.cores[r])[0], pnc=topo.addr(T.cores[r])[1]) for r in peers]
+        g.remote_dma_fused([RemoteDMATransfer(dst_ids=ids, dma_engine_mask=on_mask, remote_sem=T.sem[rsem], srcs=[ap],
+                                              dsts=[ap] * len(peers), alu_op=0)], local_sem=T.sem[lsem])
+        sent[lsem] = sent.get(lsem, 0) + ne_on
+
+    PB = [T["bank%d" % i] for i in range(8)]
+
+    dm = load("y", T.mc[:], T.mu[:], "ldm")
+    da = load("s", T.angi[:], T.ang[:], "lda")
+    dxl = load("y", T.dx[:, 64:128], T.x[:], "ldx")
+    dc = load("y", T.cnt[:], T.counts[:], "ldc")
+    ones = op("v", ms(T.rep[:], 1.0))
+    one2 = op("v", ms(T.eye[:], 1.0))
+    tails = [op("v", ms(T.D[:, 4096:4104], 1.0))]
+    for b in (T.X, T.W, T.f):
+        tails.append(op("v", ms(b[:, 4096:4104], 0.0)))
+    c_p = op("q", lambda e: e.iota(T.ip[:], [[0, 1]], 0, 1))
+    c_a = op("q", lambda e: e.iota(T.a64[:], [[2, 64]], -63, 0, allow_small_or_imprecise_dtypes=True))
+    c_b = op("q", lambda e: e.iota(T.b4i[:], [[32, 4]], 0, 0, allow_small_or_imprecise_dtypes=True))
+    c_z = op("q", lambda e: e.iota(T.ipz[:], [[-1, 16]], 0, 1))
+    c_rep = op("q", lambda e: e.affine_select(T.rep[:], T.rep[:], [[-1, 8], [0, 8], [-8, 16]], A.is_equal, 0.0, 0, 1), [ones])
+    c_eye = op("q", lambda e: e.affine_select(T.eye[:], T.eye[:], [[-1, 128]], A.is_equal, 0.0, 0, 1), [one2])
+
+    sq = [T.sq[:, 64 * i:64 * i + 64] for i in range(3)]
+    rq = [T.rq[:, 64 * i:64 * i + 64] for i in range(5)]
+    sb = [op("v", ts(sq[i], T.mc[:], QUAD[i][0], A.add), [dm]) for i in range(3)]
+    ss = [op("s", act(sq[i], sq[i], AF.Square), [sb[i]]) for i in range(3)]
+    r0 = op("v", ts(rq[0], sq[0], QUAD[0][1], A.add, -KQ, A.mult), [ss[0]])
+    r1 = op("v", ts(rq[1], sq[1], QUAD[1][1], A.add), [ss[1]])
+    r2 = op("v", ts(rq[2], sq[2], QUAD[2][1], A.add), [ss[2]])
+    r0 = op("v", tt(rq[3], rq[0], T.mc[:], A.mult), [r0])
+    r3 = op("v", tt(rq[4], rq[1], rq[2], A.mult), [r1, r2])
+    r4 = op("v", tt(sq[0], rq[4], rq[3], A.mult), [r0, r3])
+    d_c = op("v", ts(T.dx[:, 0:64], sq[0], 1.0, A.add), [r4])
+    send(partner, T.pdx[:], T.dx[:], "cx", [d_c, dxl])
+
+    def spread(src, k, deps):
+        return [[op("p", mm(PB[2 * k + half][:, 64 * h:64 * h + 64], T.rep[:, 128 * (4 * half + h):128 * (4 * half + h) + 128],
+                            src, True, True), [c_rep] + deps, 2 * k + half) for h in range(4)][-1] for half in range(2)]
+
+    def settle(win, q, k, last):
+        return [op("v", cp(win[:, 512 * q:512 * q + 256], PB[2 * k][:, 0:256]), [last[0]], 2 * k),
+                op("s", act(win[:, 512 * q + 256:512 * q + 512], PB[2 * k + 1][:, 0:256]), [last[1]], 2 * k + 1)]
+
+    m_d = spread(T.dx[:, 0:64], 0, [d_c])
+    m_x = spread(T.dx[:, 64:128], 1, [dxl])
+
+    a0 = op("v", cp(T.angf[:, 0:2], T.angi[:]), [da])
+    a1 = op("v", ts(T.ip2[:], T.ip[:], 15, A.bitwise_and), [c_p])
+    a2 = op("v", ts(T.angf[:, 2:3], T.angf[:, 1:2], -1.0, A.mult), [a0])
+    a3 = op("v", ts(T.fm[:], T.ip2[:], 2.0, A.mult, -63.0, A.add), [a1])
+    a4 = op("v", ts(T.b4[:], T.b4i[:], T.fm[:, 0:1], A.add), [a3, c_b])
+    a5 = op("v", ts(T.kc[:], T.b4[:], T.angf[:, 2:3], A.mult, 16384.0, A.add), [a4, a2])
+    a6 = op("v", ts(T.kr[:], T.b4[:], T.angf[:, 0:1], A.mult, 16384.0, A.add), [a4])
+    e_d = settle(T.D, rank, 0, m_d)
+    push(T.D[:, 512 * rank:512 * rank + 512], "pd0", "ld0", e_d)
+    for k in range(4):
+        lc = op("v", ts(T.vc[:, k:256:4], T.a64[:], T.angf[:, 0:1], A.mult, T.kc[:, k:k + 1], A.add), [a5, c_a])
+        lr = op("v", ts(T.vr[:, k:256:4], T.a64[:], T.angf[:, 1:2], A.mult, T.kr[:, k:k + 1], A.add), [a6, c_a])
+    wait("p", "cx", ne_off)
+    m_dp = spread(T.pdx[:, 0:64], 2, [])
+    m_xp = spread(T.pdx[:, 64:128], 3, [])
+    e_dp = settle(T.D, partner, 2, m_dp)
+    push(T.D[:, 512 * partner:512 * partner + 512], "pd1", "ld1", e_dp)
+    e_x = settle(T.X, rank, 1, m_x)
+    push(T.X[:, 512 * rank:512 * rank + 512], "pw0", "lw0", e_x)
+    e_xp = settle(T.X, partner, 3, m_xp)
+    push(T.X[:, 512 * partner:512 * partner + 512], "pw1", "lw1", e_xp)
+    c1 = op("v", ts(T.col[:], T.vc[:], 9, A.logical_shift_right), [lc])
+    c2 = op("v", ts(T.row[:], T.vr[:], 3, A.logical_shift_right, 0x1FFFFFC0, A.bitwise_and), [lr])
+    c5 = op("v", ts(T.tp[:], T.vr[:], 9, A.arith_shift_right), [lr])
+    c3 = op("v", ts(T.pen[:], T.col[:], 64.0, A.is_ge, 4096.0, A.mult), [c1])
+    c4 = op("v", tt(T.raw[:], T.col[:], T.row[:], A.add), [c1, c2])
+    tl = op("v", ts(T.tl[:], T.tp[:], 0.0, A.max, 63.0, A.min), [c5])
+    c6 = op("v", tt(T.raw2[:], T.raw[:], T.pen[:], A.add), [c3, c4])
+    fl = op("v", ts(T.fl[:], T.raw2[:], 4096.0, A.min), [c6])
+    s_1 = op("v", ts(T.ipz2[:], T.ipz[:], 15, A.bitwise_and), [c_z])
+    s_sel = op("v", ts(T.ssel[:], T.ipz[:], 0.0, A.is_equal, 2048.0, A.mult), [c_z])
+    s_sum = op("v", ts(T.ssum[:], T.ipz2[:], 0.0, A.is_equal), [s_1])
+    zz = op("v", ms(T.z0[:], 0.0))
+
+    Ew = T.e[:, 0:64]
+
+    def gath(eng, out, win, off, deps):
+        src = win.indirect(off)
+        return op(eng, cp(out, src) if eng == "v" else act(out, src), deps)
+
+    for eng in ("s", "v"):
+        wait(eng, "pd0", npush)
+        wait(eng, "pd1", npush)
+    DCH = [("v", 48, 64), ("s", 0, 16), ("s", 16, 32), ("s", 32, 48)]
+    dg = {}
+    for eng, a, z in DCH:
+        dg[a] = gath(eng, T.f[:, 64 * a:64 * z], T.D[:], T.fl[:, 4 * a:4 * z], [fl] + e_d + e_dp + tails)
+    wsc = []
+    for _, a, z in DCH[1:] + DCH[:1]:
+        h0 = op("v", cp(T.z0[:, 64 * a:64 * z:64], T.f[:, 64 * a:64 * z:64]), [dg[a], zz])
+        h1 = op("v", ms(T.f[:, 64 * a:64 * z:64], 0.0), [h0])
+        wsc.append(op("v", scan(T.W[:, 64 * a:64 * z], T.f[:, 64 * a:64 * z], T.z0[:, 64 * a:64 * z]), [h1]))
+
+    def order(k):
+        return [(s, [members[s][(me + 1 + n) % NQ] for n in range(NQ)]) for s in ([0, 1] if k < R - 1 else [1 - ci, ci])]
+
+    seq0 = [q for s, bl in order(0) for q in bl]
+    bank_of = {}
+    for n, q in enumerate(seq0):
+        if n % NQ:
+            bank_of[q] = 2 + len(bank_of)
+
+    def hscan(a, z, dep):
+        lo = 64 * a - 1 if a else None
+        return op("v", scan(T.st[:, 64 * z - 1:lo:-1], T.f[:, 64 * z:64 * a:-1], T.xg[:, 64 * z - 1:lo:-1]), [dep])
+
+    wbg, loc = {}, {}
+    ev = e_x + e_xp
+    for k in range(R):
+        last = k == R - 1
+        for eng in ("s", "v"):
+            for n in (("pw0", "pw1") if k == 0 else ("pu_%d_0" % (k - 1), "pu_%d_1" % (k - 1))):
+                wait(eng, n, npush)
+
+        def xgath(eng, a, z):
+            return (a, z, gath(eng, T.xg[:, 64 * a:64 * z], T.X[:], T.fl[:, 4 * a:4 * z], ev + tails))
+
+        if k == 0:
+            sc = [xgath("s", a, a + 16) for a in range(0, 64, 16)]
+            for n, q in enumerate(seq0):
+                wbg[q] = gath("v" if n < 5 else "s", T.wb[:, 512 * q:512 * q + 512], T.W[:], T.fl[:, 32 * q:32 * q + 32],
+                              wsc + tails)
+            hs = [hscan(*c) for c in sc]
+        else:
+            sc = [xgath("s", a, z) for a, z in ((12, 24), (24, 36), (36, 48), (48, 58), (58, 64))]
+            va = xgath("v", 0, 8)
+            hs = [hscan(*va), hscan(*sc[0])]
+            vb = xgath("v", 8, 12)
+            hs += [hscan(*c) for c in [sc[1], vb] + sc[2:]]
+        e0 = op("v", tt(T.u[:], T.z0[:, 0:4096:64], T.st[:, 0:4096:64], A.mult), hs)
+        ee = op("v", tt(T.e[:], T.cnt[:], T.u[:], A.subtract), [e0, dc])
+
+        ordr = order(k)
+        seq = [(s, q) for s, bl in ordr for q in bl]
+        egd, bsum, part = {}, {}, {}
+        for s, q in seq:
+            if q in bank_of:
+                b = bank_of[q]
+                if k == 0:
+                    loc[q] = op("s", act(PB[b][:], T.wb[:, 512 * q:512 * q + 512]), [wbg[q]], b)
+                egd[q] = gath("s", T.eg[:, 512 * (b - 2):512 * (b - 1)], Ew, T.tl[:, 32 * q:32 * q + 32], [ee, tl])
+
+        def evac(n):
+            q = seq[n][1]
+            o = T.snd[:, 64 * (k * 8 + n):64 * (k * 8 + n) + 64]
+            part[q] = (o, op("v", cp(o, PB[n % 2][:, 0:64]), [bsum[q]], n % 2))
+
+        for n, (s, q) in enumerate(seq):
+            out = T.pr[:, 512 * q:512 * q + 512]
+            if q in bank_of:
+                b = bank_of[q]
+                pd = op("v", tt(out, T.eg[:, 512 * (b - 2):512 * (b - 1)], PB[b][:], A.mult), [egd[q], loc[q]], b)
+            else:
+                pd = op("v", tt(out, Ew.indirect(T.tl[:, 32 * q:32 * q + 32]), T.wb[:, 512 * q:512 * q + 512], A.mult),
+                        [ee, wbg[q], tl])
+            own = q in (rank, partner)
+            for b in range(4):
+                o = PB[n % 2][:, b:64:4]
+                px = slice(512 * q + 128 * b, 512 * q + 128 * b + 128)
+                if own:
+                    op("p", mm(o, T.X[:, px], T.ssel[:], True, False), [s_sel] + ev, n % 2)
+                bsum[q] = op("p", mm(o, T.pr[:, px], T.ssum[:], not own, True), [pd, s_sum], n % 2)
+            if n:
+                evac(n - 1)
+        evac(len(seq) - 1)
+        for s, q in seq:
+            i = (members[s].index(q) - me) % NQ
+            if i:
+                col = 64 * ((k * 2 + s) * 3 + i - 1)
+                send(mine[(me + i) % NQ], T.lnd[:, col:col + 64], part[q][0], "rs_%d_%d" % (k, s), [part[q][1]])
+
+        pts = {}
+        for s, bl in ordr:
+            q, m = bl[-1], 64 * (k * 2 + s)
+            wait("v", "rs_%d_%d" % (k, s), npush)
+            a = op("v", tt(T.t1[:], T.lnd[:, 3 * m:3 * m + 64], T.lnd[:, 3 * m + 64:3 * m + 128], A.add), [hist.get("pt")])
+            b = op("v", tt(T.t2[:], T.lnd[:, 3 * m + 128:3 * m + 192], part[q][0], A.add), [part[q][1]])
+            hist["pt"] = pts[s] = op("v", tt(T.pt[:, m:m + 64], T.t1[:], T.t2[:], A.add), [a, b])
+            if not last or s != ci:
+                send(partner, T.xs[:, m:m + 64], T.pt[:, m:m + 64], "xc_%d_%d" % (k, s), [pts[s]])
+        evs = []
+        for s, bl in ordr:
+            if last and s != ci:
+                continue
+            q, m = bl[-1], 64 * (k * 2 + s)
+            wait("v", "xc_%d_%d" % (k, s), ne_off)
+            r = 512 * s
+            n = op("v", tt(T.rp[:, r:r + 64], T.pt[:, m:m + 64], T.xs[:, m:m + 64], A.add), [pts[s], hist.get(s)])
+            if last:
+                for b in range(4):
+                    hist[s] = op("p", mm(PB[0][0:16, 128 * b:128 * b + 128], T.rp[:, r + b:r + 64:4], T.eye[:], True, True),
+                                 [n, c_eye], 0)
+                waits("y", [op("v", ts(T.ysb[0:16, :], PB[0][0:16, :], STEP, A.mult, 0.0, A.max), [hist[s]], 0)])
+                load("y", T.y[:], T.ysb[0:16, :], "yo")
+                continue
+            cps = [n]
+            for j in range(1, 8):
+                o, i = T.rp[:, r + 64 * j:r + 64 * j + 64], T.rp[:, r:r + 64]
+                cps.append(op("v", cp(o, i), [n]) if j < 4 else op("s", act(o, i), [n]))
+            tp = [op("p", mm(PB[b // 2][:, 128 * (b % 2):128 * (b % 2) + 128], T.rp[:, r + b:r + 512:4], T.eye[:], True, True),
+                     cps + [c_eye], b // 2) for b in range(4)]
+            hist[s] = tp[3]
+            for eng in ("v", "s"):
+                for n in (["lp_%d_%d" % (k - 1, s)] if k else ["lw0", "lw1"]):
+                    wait(eng, n, ne_on)
+            ab = [op("v", ts(T.X[:, 512 * q:512 * q + 256], PB[0][:, 0:256], STEP, A.mult, 0.0, A.max), [tp[1]], 0),
+                  op("s", act(T.X[:, 512 * q + 256:512 * q + 512], PB[1][:, 0:256], AF.Relu, STEP), [tp[3]], 1)]
+            push(T.X[:, 512 * q:512 * q + 512], "pu_%d_%d" % (k, s), "lp_%d_%d" % (k, s), ab)
+            evs += ab
+        ev = evs
+
+    for e in ("v", "s", "p", "q"):
+        wait("q", e, cnt[e])
+    for n in sorted(sent):
+        wait("q", n, sent[n])
+    for n in ("ldm", "ldx", "lda", "ldc", "yo"):
+        wait("q", n, 16)

@@ -3,15 +3,18 @@ from concourse.mybir import AluOpType as A, ActivationFunctionType as AF
 
 R = 3
 STEP = 2.0 ** -12
+STAGES = [(0, 0, 512), (1, 0, 512)]
+LAG = 2048
+WBV = 6
 KQ = 0.00012918686694904754
 QUAD = [(1.1219518404595346, 18.754011438386996), (-4.267052247540635, 2.746736091488364),
         (-1.8906565018022652, 14.883958171039492)]
 SCRATCH = {}
 for _n, _w in (("mc", 64), ("dx", 128), ("pdx", 128), ("angf", 4), ("cnt", 64), ("sq", 192), ("rq", 320), ("rep", 1024),
                ("eye", 128), ("ssum", 16), ("ssel", 16), ("fm", 1), ("a64", 64), ("b4i", 4), ("b4", 4), ("kc", 4), ("kr", 4),
-               ("pen", 256), ("raw", 256), ("raw2", 256), ("D", 4104), ("X", 4104), ("W", 4104), ("f", 4104), ("z0", 4096),
+               ("pen", 256), ("raw", 256), ("raw2", 256), ("D", 4104), ("X", 4104), ("W", 4104), ("f", 4104), ("ind", 1024),
                ("xg", 4096), ("st", 4096), ("wb", 4096), ("pr", 4096), ("eg", 3072), ("u", 64), ("e", 64), ("snd", 1536),
-               ("lnd", 1152), ("t1", 64), ("t2", 64), ("pt", 384), ("xs", 384), ("rp", 1024), ("ysb", 512)):
+               ("lnd", 1152), ("t1", 64), ("t2", 64), ("pt", 384), ("xs", 384), ("rp", 1024), ("ysb", 512), ("d0", 64)):
     SCRATCH[_n] = ("sbuf", [128, _w], "float32")
 for _n, _w in (("angi", 2), ("ipz", 16), ("ipz2", 16), ("ip", 1), ("ip2", 1), ("vc", 256), ("vr", 256), ("col", 256),
                ("row", 256), ("tp", 256)):
@@ -20,9 +23,9 @@ for _n in ("fl", "tl"):
     SCRATCH[_n] = ("sbuf", [128, 256], "uint16")
 for _n in range(8):
     SCRATCH["bank%d" % _n] = ("psum", [128, 512], "float32")
-SEMAPHORES = (["v", "s", "p", "q", "ldm", "ldx", "lda", "ldc", "yo", "cx", "lr"]
+SEMAPHORES = (["v", "s", "p", "q", "ldm", "ldx", "lda", "ldc", "yo", "cx", "cd", "lr"]
               + ["pd0", "pd1", "pw0", "pw1", "ld0", "ld1", "lw0", "lw1"]
-              + ["%s_%d_%d" % (n, k, s) for n in ("rs", "xc", "pu", "lp") for k in range(R) for s in range(2)])
+              + ["%s_%d_%d" % (n, k, s) for n in ("rs", "xc", "pu", "lp") for k in range(R) for s in range(len(STAGES))])
 
 
 def ts(out, i, s1, o0, s2=None, o1=None):
@@ -51,8 +54,8 @@ def ms(ap, c):
     return lambda e: e.memset(ap, c)
 
 
-def scan(out, d0, d1):
-    return lambda e: e.tensor_tensor_scan(out, d0, d1, 0.0, A.mult, A.add)
+def scan(out, d0, d1, o0=A.mult, o1=A.add):
+    return lambda e: e.tensor_tensor_scan(out, d0, d1, 0.0, o0, o1)
 
 
 def rank_program(g, core, T, topo):
@@ -101,7 +104,8 @@ def rank_program(g, core, T, topo):
 
     def load(eng, out, in_, sem):
         ENG[eng].dma_start(out, in_).then_inc(T.sem[sem], 16)
-        return (sem, 16)
+        hist[sem] = hist.get(sem, 0) + 16
+        return (sem, hist[sem])
 
     def send(dst, out, in_, rsem, deps):
         waits("q", deps)
@@ -120,8 +124,8 @@ def rank_program(g, core, T, topo):
     PB = [T["bank%d" % i] for i in range(8)]
 
     dm = load("y", T.mc[:], T.mu[:], "ldm")
-    da = load("s", T.angi[:], T.ang[:], "lda")
-    dxl = load("y", T.dx[:, 64:128], T.x[:], "ldx")
+    dxl = load("s", T.dx[:, 64:128], T.x[:], "ldx")
+    da = load("y", T.angi[:], T.ang[:], "lda")
     dc = load("y", T.cnt[:], T.counts[:], "ldc")
     ones = op("v", ms(T.rep[:], 1.0))
     one2 = op("v", ms(T.eye[:], 1.0))
@@ -133,7 +137,7 @@ def rank_program(g, core, T, topo):
     c_b = op("q", lambda e: e.iota(T.b4i[:], [[32, 4]], 0, 0, allow_small_or_imprecise_dtypes=True))
     c_z = op("q", lambda e: e.iota(T.ipz[:], [[-1, 16]], 0, 1))
     c_rep = op("q", lambda e: e.affine_select(T.rep[:], T.rep[:], [[-1, 8], [0, 8], [-8, 16]], A.is_equal, 0.0, 0, 1), [ones])
-    c_eye = op("q", lambda e: e.affine_select(T.eye[:], T.eye[:], [[-1, 128]], A.is_equal, 0.0, 0, 1), [one2])
+    send(partner, T.pdx[:, 64:128], T.dx[:, 64:128], "cx", [dxl])
 
     sq = [T.sq[:, 64 * i:64 * i + 64] for i in range(3)]
     rq = [T.rq[:, 64 * i:64 * i + 64] for i in range(5)]
@@ -146,7 +150,8 @@ def rank_program(g, core, T, topo):
     r3 = op("v", tt(rq[4], rq[1], rq[2], A.mult), [r1, r2])
     r4 = op("v", tt(sq[0], rq[4], rq[3], A.mult), [r0, r3])
     d_c = op("v", ts(T.dx[:, 0:64], sq[0], 1.0, A.add), [r4])
-    send(partner, T.pdx[:], T.dx[:], "cx", [d_c, dxl])
+    send(partner, T.pdx[:, 0:64], T.dx[:, 0:64], "cd", [d_c])
+    c_eye = op("q", lambda e: e.affine_select(T.eye[:], T.eye[:], [[-1, 128]], A.is_equal, 0.0, 0, 1), [one2])
 
     def spread(src, k, deps):
         return [[op("p", mm(PB[2 * k + half][:, 64 * h:64 * h + 64], T.rep[:, 128 * (4 * half + h):128 * (4 * half + h) + 128],
@@ -171,8 +176,11 @@ def rank_program(g, core, T, topo):
     for k in range(4):
         lc = op("v", ts(T.vc[:, k:256:4], T.a64[:], T.angf[:, 0:1], A.mult, T.kc[:, k:k + 1], A.add), [a5, c_a])
         lr = op("v", ts(T.vr[:, k:256:4], T.a64[:], T.angf[:, 1:2], A.mult, T.kr[:, k:k + 1], A.add), [a6, c_a])
-    wait("p", "cx", ne_off)
+    c1 = op("v", ts(T.col[:], T.vc[:], 9, A.logical_shift_right), [lc])
+    c2 = op("v", ts(T.row[:], T.vr[:], 3, A.logical_shift_right, 0x1FFFFFC0, A.bitwise_and), [lr])
+    wait("p", "cd", ne_off)
     m_dp = spread(T.pdx[:, 0:64], 2, [])
+    wait("p", "cx", ne_off)
     m_xp = spread(T.pdx[:, 64:128], 3, [])
     e_dp = settle(T.D, partner, 2, m_dp)
     push(T.D[:, 512 * partner:512 * partner + 512], "pd1", "ld1", e_dp)
@@ -180,18 +188,17 @@ def rank_program(g, core, T, topo):
     push(T.X[:, 512 * rank:512 * rank + 512], "pw0", "lw0", e_x)
     e_xp = settle(T.X, partner, 3, m_xp)
     push(T.X[:, 512 * partner:512 * partner + 512], "pw1", "lw1", e_xp)
-    c1 = op("v", ts(T.col[:], T.vc[:], 9, A.logical_shift_right), [lc])
-    c2 = op("v", ts(T.row[:], T.vr[:], 3, A.logical_shift_right, 0x1FFFFFC0, A.bitwise_and), [lr])
-    c5 = op("v", ts(T.tp[:], T.vr[:], 9, A.arith_shift_right), [lr])
     c3 = op("v", ts(T.pen[:], T.col[:], 64.0, A.is_ge, 4096.0, A.mult), [c1])
     c4 = op("v", tt(T.raw[:], T.col[:], T.row[:], A.add), [c1, c2])
-    tl = op("v", ts(T.tl[:], T.tp[:], 0.0, A.max, 63.0, A.min), [c5])
+    c5 = op("v", ts(T.tp[:], T.vr[:], 9, A.arith_shift_right), [lr])
     c6 = op("v", tt(T.raw2[:], T.raw[:], T.pen[:], A.add), [c3, c4])
     fl = op("v", ts(T.fl[:], T.raw2[:], 4096.0, A.min), [c6])
+    tl = op("v", ts(T.tl[:], T.tp[:], 0.0, A.max, 63.0, A.min), [c5])
     s_1 = op("v", ts(T.ipz2[:], T.ipz[:], 15, A.bitwise_and), [c_z])
     s_sel = op("v", ts(T.ssel[:], T.ipz[:], 0.0, A.is_equal, 2048.0, A.mult), [c_z])
     s_sum = op("v", ts(T.ssum[:], T.ipz2[:], 0.0, A.is_equal), [s_1])
-    zz = op("v", ms(T.z0[:], 0.0))
+    in0 = op("v", ms(T.ind[:], 0.0))
+    in1 = op("v", ms(T.ind[:, 0:1024:64], 1.0), [in0])
 
     Ew = T.e[:, 0:64]
 
@@ -207,127 +214,164 @@ def rank_program(g, core, T, topo):
     for eng, a, z in DCH:
         dg[a] = gath(eng, T.f[:, 64 * a:64 * z], T.D[:], T.fl[:, 4 * a:4 * z], [fl] + e_d + e_dp + tails)
     wsc = []
-    for _, a, z in DCH[1:] + DCH[:1]:
-        h0 = op("v", cp(T.z0[:, 64 * a:64 * z:64], T.f[:, 64 * a:64 * z:64]), [dg[a], zz])
-        h1 = op("v", ms(T.f[:, 64 * a:64 * z:64], 0.0), [h0])
-        wsc.append(op("v", scan(T.W[:, 64 * a:64 * z], T.f[:, 64 * a:64 * z], T.z0[:, 64 * a:64 * z]), [h1]))
+    for _, a, z in DCH:
+        wsc.append(op("v", scan(T.W[:, 64 * a:64 * z], T.ind[:], T.f[:, 64 * a:64 * z], A.max, A.mult), [dg[a], in1]))
+    d0 = op("v", cp(T.d0[:], T.f[:, 0:4096:64]), wsc)
+    fz = op("v", ms(T.f[:, 0:4096:64], 0.0), [d0])
 
     def order(k):
-        return [(s, [members[s][(me + 1 + n) % NQ] for n in range(NQ)]) for s in ([0, 1] if k < R - 1 else [1 - ci, ci])]
+        idx = list(range(len(STAGES)))
+        if k == R - 1:
+            idx.sort(key=lambda i: STAGES[i][0] == ci)
+        return idx
 
-    seq0 = [q for s, bl in order(0) for q in bl]
-    bank_of = {}
-    for n, q in enumerate(seq0):
-        if n % NQ:
-            bank_of[q] = 2 + len(bank_of)
+    def chunk(i, n):
+        s, lo, hi = STAGES[i]
+        return 512 * members[s][(me + 1 + n) % NQ] + lo, hi - lo
+
+    at, room = {}, 0
+    for i in order(0):
+        for n in range(1, NQ):
+            at[(i, n)] = room
+            room += chunk(i, n)[1]
+    soff = [sum(h - l for _, l, h in STAGES[:i]) // 8 for i in range(len(STAGES))]
 
     def hscan(a, z, dep):
         lo = 64 * a - 1 if a else None
-        return op("v", scan(T.st[:, 64 * z - 1:lo:-1], T.f[:, 64 * z:64 * a:-1], T.xg[:, 64 * z - 1:lo:-1]), [dep])
+        return op("v", scan(T.st[:, 64 * z - 1:lo:-1], T.f[:, 64 * z:64 * a:-1], T.xg[:, 64 * z - 1:lo:-1]), [dep, fz])
 
-    wbg, loc = {}, {}
+    wbg, loc, run = {}, {}, [0]
     ev = e_x + e_xp
     for k in range(R):
         last = k == R - 1
         for eng in ("s", "v"):
-            for n in (("pw0", "pw1") if k == 0 else ("pu_%d_0" % (k - 1), "pu_%d_1" % (k - 1))):
+            for n in (("pw0", "pw1") if k == 0 else ["pu_%d_%d" % (k - 1, i) for i in range(len(STAGES))]):
                 wait(eng, n, npush)
 
         def xgath(eng, a, z):
             return (a, z, gath(eng, T.xg[:, 64 * a:64 * z], T.X[:], T.fl[:, 4 * a:4 * z], ev + tails))
 
+        ordr = order(k)
+        seq = [(i, n) for i in ordr for n in range(NQ)]
         if k == 0:
             sc = [xgath("s", a, a + 16) for a in range(0, 64, 16)]
-            for n, q in enumerate(seq0):
-                wbg[q] = gath("v" if n < 5 else "s", T.wb[:, 512 * q:512 * q + 512], T.W[:], T.fl[:, 32 * q:32 * q + 32],
+            done = 0
+            for c in seq:
+                p, w = chunk(*c)
+                wbg[c] = gath("v" if done < 512 * WBV else "s", T.wb[:, p:p + w], T.W[:], T.fl[:, p // 16:(p + w) // 16],
                               wsc + tails)
+                done += w
             hs = [hscan(*c) for c in sc]
         else:
-            sc = [xgath("s", a, z) for a, z in ((12, 24), (24, 36), (36, 48), (48, 58), (58, 64))]
+            sc = [xgath("s", a, z) for a, z in ((14, 26), (26, 38), (38, 50), (50, 60), (60, 64))]
             va = xgath("v", 0, 8)
             hs = [hscan(*va), hscan(*sc[0])]
-            vb = xgath("v", 8, 12)
+            vb = xgath("v", 8, 14)
             hs += [hscan(*c) for c in [sc[1], vb] + sc[2:]]
-        e0 = op("v", tt(T.u[:], T.z0[:, 0:4096:64], T.st[:, 0:4096:64], A.mult), hs)
+        e0 = op("v", tt(T.u[:], T.d0[:], T.st[:, 0:4096:64], A.mult), hs + [d0])
         ee = op("v", tt(T.e[:], T.cnt[:], T.u[:], A.subtract), [e0, dc])
 
-        ordr = order(k)
-        seq = [(s, q) for s, bl in ordr for q in bl]
+        def place(c):
+            p, w = chunk(*c)
+            loc[c] = op("s", act(PB[2 + at[c] // 512][:, at[c] % 512:at[c] % 512 + w], T.wb[:, p:p + w]), [wbg[c]],
+                        2 + at[c] // 512)
+
         egd, bsum, part = {}, {}, {}
-        for s, q in seq:
-            if q in bank_of:
-                b = bank_of[q]
-                if k == 0:
-                    loc[q] = op("s", act(PB[b][:], T.wb[:, 512 * q:512 * q + 512]), [wbg[q]], b)
-                egd[q] = gath("s", T.eg[:, 512 * (b - 2):512 * (b - 1)], Ew, T.tl[:, 32 * q:32 * q + 32], [ee, tl])
+        inp = [c for c in seq if c in at]
+        if k == 0:
+            for c in inp[:4]:
+                place(c)
+        for c in inp:
+            if c not in loc:
+                place(c)
+            p, w = chunk(*c)
+            egd[c] = gath("s", T.eg[:, at[c]:at[c] + w], Ew, T.tl[:, p // 16:(p + w) // 16], [ee, tl])
 
         def evac(n):
-            q = seq[n][1]
-            o = T.snd[:, 64 * (k * 8 + n):64 * (k * 8 + n) + 64]
-            part[q] = (o, op("v", cp(o, PB[n % 2][:, 0:64]), [bsum[q]], n % 2))
-
-        for n, (s, q) in enumerate(seq):
-            out = T.pr[:, 512 * q:512 * q + 512]
-            if q in bank_of:
-                b = bank_of[q]
-                pd = op("v", tt(out, T.eg[:, 512 * (b - 2):512 * (b - 1)], PB[b][:], A.mult), [egd[q], loc[q]], b)
-            else:
-                pd = op("v", tt(out, Ew.indirect(T.tl[:, 32 * q:32 * q + 32]), T.wb[:, 512 * q:512 * q + 512], A.mult),
-                        [ee, wbg[q], tl])
-            own = q in (rank, partner)
-            for b in range(4):
-                o = PB[n % 2][:, b:64:4]
-                px = slice(512 * q + 128 * b, 512 * q + 128 * b + 128)
-                if own:
-                    op("p", mm(o, T.X[:, px], T.ssel[:], True, False), [s_sel] + ev, n % 2)
-                bsum[q] = op("p", mm(o, T.pr[:, px], T.ssum[:], not own, True), [pd, s_sum], n % 2)
-            if n:
-                evac(n - 1)
-        evac(len(seq) - 1)
-        for s, q in seq:
-            i = (members[s].index(q) - me) % NQ
-            if i:
-                col = 64 * ((k * 2 + s) * 3 + i - 1)
-                send(mine[(me + i) % NQ], T.lnd[:, col:col + 64], part[q][0], "rs_%d_%d" % (k, s), [part[q][1]])
+            c = seq[n]
+            w = chunk(*c)[1] // 8
+            o = T.snd[:, run[0]:run[0] + w]
+            run[0] += w
+            part[c] = (o, op("v", cp(o, PB[n % 2][:, 0:w]), [bsum[c]], n % 2))
 
         pts = {}
-        for s, bl in ordr:
-            q, m = bl[-1], 64 * (k * 2 + s)
-            wait("v", "rs_%d_%d" % (k, s), npush)
-            a = op("v", tt(T.t1[:], T.lnd[:, 3 * m:3 * m + 64], T.lnd[:, 3 * m + 64:3 * m + 128], A.add), [hist.get("pt")])
-            b = op("v", tt(T.t2[:], T.lnd[:, 3 * m + 128:3 * m + 192], part[q][0], A.add), [part[q][1]])
-            hist["pt"] = pts[s] = op("v", tt(T.pt[:, m:m + 64], T.t1[:], T.t2[:], A.add), [a, b])
-            if not last or s != ci:
-                send(partner, T.xs[:, m:m + 64], T.pt[:, m:m + 64], "xc_%d_%d" % (k, s), [pts[s]])
+
+        def chipsum(i):
+            w = chunk(i, 0)[1] // 8
+            m = 128 * k + soff[i]
+            wait("v", "rs_%d_%d" % (k, i), npush)
+            a = op("v", tt(T.t1[:, 0:w], T.lnd[:, 3 * m:3 * m + w], T.lnd[:, 3 * m + w:3 * m + 2 * w], A.add), [hist.get("pt")])
+            o, d = part[(i, NQ - 1)]
+            b = op("v", tt(T.t2[:, 0:w], T.lnd[:, 3 * m + 2 * w:3 * m + 3 * w], o, A.add), [d])
+            hist["pt"] = pts[i] = op("v", tt(T.pt[:, m:m + w], T.t1[:, 0:w], T.t2[:, 0:w], A.add), [a, b])
+
+        due, todo = {}, list(ordr)
+        for n, c in enumerate(seq):
+            p, w = chunk(*c)
+            out = T.pr[:, p:p + w]
+            if c in at:
+                b, r = 2 + at[c] // 512, at[c] % 512
+                pd = op("v", tt(out, T.eg[:, at[c]:at[c] + w], PB[b][:, r:r + w], A.mult), [egd[c], loc[c]], b)
+            else:
+                pd = op("v", tt(out, Ew.indirect(T.tl[:, p // 16:(p + w) // 16]), T.wb[:, p:p + w], A.mult), [ee, wbg[c], tl])
+            own = c[1] == NQ - 1
+            nb = w // 128
+            for b in range(nb):
+                o = PB[n % 2][:, b:16 * nb:nb]
+                px = slice(p + 128 * b, p + 128 * b + 128)
+                if own:
+                    op("p", mm(o, T.X[:, px], T.ssel[:], True, False), [s_sel] + ev, n % 2)
+                bsum[c] = op("p", mm(o, T.pr[:, px], T.ssum[:], not own, True), [pd, s_sum], n % 2)
+            if n:
+                evac(n - 1)
+            for i in due:
+                due[i] += w
+            if own:
+                due[c[0]] = 0
+            while due.get(todo[0], -1) >= LAG:
+                chipsum(todo.pop(0))
+        evac(len(seq) - 1)
+        for i in todo:
+            chipsum(i)
+        for c in seq:
+            p, w = chunk(*c)
+            if c[1] < NQ - 1:
+                m = 3 * (128 * k + soff[c[0]]) + c[1] * w // 8
+                send(peers[c[1]], T.lnd[:, m:m + w // 8], part[c][0], "rs_%d_%d" % (k, c[0]), [part[c][1]])
+        for i in ordr:
+            m, w = 128 * k + soff[i], chunk(i, 0)[1] // 8
+            if not last or STAGES[i][0] != ci:
+                send(partner, T.xs[:, m:m + w], T.pt[:, m:m + w], "xc_%d_%d" % (k, i), [pts[i]])
+
         evs = []
-        for s, bl in ordr:
-            if last and s != ci:
+        for i in ordr:
+            if last and STAGES[i][0] != ci:
                 continue
-            q, m = bl[-1], 64 * (k * 2 + s)
-            wait("v", "xc_%d_%d" % (k, s), ne_off)
-            r = 512 * s
-            n = op("v", tt(T.rp[:, r:r + 64], T.pt[:, m:m + 64], T.xs[:, m:m + 64], A.add), [pts[s], hist.get(s)])
+            p, w = chunk(i, NQ - 1)
+            nb, w8, m, r, h = w // 128, w // 8, 128 * k + soff[i], 8 * soff[i], w // 2
+            wait("v", "xc_%d_%d" % (k, i), ne_off)
+            n = op("v", tt(T.rp[:, r:r + w8], T.pt[:, m:m + w8], T.xs[:, m:m + w8], A.add), [pts[i], hist.get(i)])
+            cps, rows, win, lo = [n], 16, T.ysb, p % 512
+            if not last:
+                rows, win, lo = 128, T.X, p
+                for j in range(1, 8):
+                    o, f = T.rp[:, r + w8 * j:r + w8 * j + w8], T.rp[:, r:r + w8]
+                    cps.append(op("v", cp(o, f), [n]) if j < 4 else op("s", act(o, f), [n]))
+                for eng in ("v", "s"):
+                    for b in (["lp_%d_%d" % (k - 1, i)] if k else ["lw0", "lw1"]):
+                        wait(eng, b, ne_on)
+            hb = nb // 2
+            tp = [op("p", mm(PB[b // hb][0:rows, 128 * (b % hb):128 * (b % hb) + 128], T.rp[:, r + b:r + rows * nb:nb], T.eye[:],
+                             True, True), cps + [c_eye], b // hb) for b in range(nb)]
+            hist[i] = tp[-1]
+            ab = [op("v", ts(win[0:rows, lo:lo + h], PB[0][0:rows, 0:h], STEP, A.mult, 0.0, A.max), [tp[hb - 1]], 0),
+                  op("s", act(win[0:rows, lo + h:lo + w], PB[1][0:rows, 0:h], AF.Relu, STEP), [tp[-1]], 1)]
             if last:
-                for b in range(4):
-                    hist[s] = op("p", mm(PB[0][0:16, 128 * b:128 * b + 128], T.rp[:, r + b:r + 64:4], T.eye[:], True, True),
-                                 [n, c_eye], 0)
-                waits("y", [op("v", ts(T.ysb[0:16, :], PB[0][0:16, :], STEP, A.mult, 0.0, A.max), [hist[s]], 0)])
-                load("y", T.y[:], T.ysb[0:16, :], "yo")
-                continue
-            cps = [n]
-            for j in range(1, 8):
-                o, i = T.rp[:, r + 64 * j:r + 64 * j + 64], T.rp[:, r:r + 64]
-                cps.append(op("v", cp(o, i), [n]) if j < 4 else op("s", act(o, i), [n]))
-            tp = [op("p", mm(PB[b // 2][:, 128 * (b % 2):128 * (b % 2) + 128], T.rp[:, r + b:r + 512:4], T.eye[:], True, True),
-                     cps + [c_eye], b // 2) for b in range(4)]
-            hist[s] = tp[3]
-            for eng in ("v", "s"):
-                for n in (["lp_%d_%d" % (k - 1, s)] if k else ["lw0", "lw1"]):
-                    wait(eng, n, ne_on)
-            ab = [op("v", ts(T.X[:, 512 * q:512 * q + 256], PB[0][:, 0:256], STEP, A.mult, 0.0, A.max), [tp[1]], 0),
-                  op("s", act(T.X[:, 512 * q + 256:512 * q + 512], PB[1][:, 0:256], AF.Relu, STEP), [tp[3]], 1)]
-            push(T.X[:, 512 * q:512 * q + 512], "pu_%d_%d" % (k, s), "lp_%d_%d" % (k, s), ab)
-            evs += ab
+                waits("y", ab)
+                load("y", T.y[:, lo:lo + w], T.ysb[0:16, lo:lo + w], "yo")
+            else:
+                push(T.X[:, p:p + w], "pu_%d_%d" % (k, i), "lp_%d_%d" % (k, i), ab)
+                evs += ab
         ev = evs
 
     for e in ("v", "s", "p", "q"):
@@ -335,4 +379,4 @@ def rank_program(g, core, T, topo):
     for n in sorted(sent):
         wait("q", n, sent[n])
     for n in ("ldm", "ldx", "lda", "ldc", "yo"):
-        wait("q", n, 16)
+        wait("q", n, hist[n])

@@ -4,17 +4,21 @@ from concourse.mybir import AluOpType as A, ActivationFunctionType as AF
 R = 3
 STEP = 2.0 ** -12
 STAGES = [(0, 0, 512), (1, 0, 512)]
-LAG = 2048
-WBV = 6
+LAG = 1536
+WBV = 5
+PLP = 3
+DCH = [("v", 52, 64), ("s", 0, 14), ("s", 14, 28), ("s", 28, 42), ("s", 42, 52)]
+TAIL = [("c", 0), ("c", 1), ("n", 0), ("n", 1)]
 KQ = 0.00012918686694904754
 QUAD = [(1.1219518404595346, 18.754011438386996), (-4.267052247540635, 2.746736091488364),
         (-1.8906565018022652, 14.883958171039492)]
 SCRATCH = {}
-for _n, _w in (("mc", 64), ("dx", 128), ("pdx", 128), ("angf", 4), ("cnt", 64), ("sq", 192), ("rq", 320), ("rep", 1024),
-               ("eye", 128), ("ssum", 16), ("ssel", 16), ("fm", 1), ("a64", 64), ("b4i", 4), ("b4", 4), ("kc", 4), ("kr", 4),
-               ("pen", 256), ("raw", 256), ("raw2", 256), ("D", 4104), ("X", 4104), ("W", 4104), ("f", 4104), ("ind", 1024),
-               ("xg", 4096), ("st", 4096), ("wb", 4096), ("pr", 4096), ("eg", 3072), ("u", 64), ("e", 64), ("snd", 1536),
-               ("lnd", 1152), ("t1", 64), ("t2", 64), ("pt", 384), ("xs", 384), ("rp", 1024), ("ysb", 512), ("d0", 64)):
+for _n, _w in (("mc", 64), ("dx", 128), ("pdx", 128), ("angf", 4), ("cnt", 64), ("sq", 192), ("rq", 320),
+               ("rep", 1024), ("ssum", 16), ("ssel", 16), ("fm", 1), ("a64", 64), ("b4i", 4), ("b4", 4), ("kc", 4),
+               ("kr", 4), ("pen", 256), ("raw", 256), ("raw2", 256), ("D", 4104), ("X", 4104), ("W", 4104), ("f", 4104),
+               ("ind", 1024), ("xg", 4096), ("st", 4096), ("wb", 4096), ("pr", 4096), ("eg", 3072), ("u", 64), ("e", 64),
+               ("snd", 1536), ("lnd", 1152), ("t1", 64), ("t2", 64), ("pt", 384), ("xs", 384), ("rp", 1024), ("ysb", 512),
+               ("d0", 64), ("old", 128)):
     SCRATCH[_n] = ("sbuf", [128, _w], "float32")
 for _n, _w in (("angi", 2), ("ipz", 16), ("ipz2", 16), ("ip", 1), ("ip2", 1), ("vc", 256), ("vr", 256), ("col", 256),
                ("row", 256), ("tp", 256)):
@@ -71,6 +75,7 @@ def rank_program(g, core, T, topo):
     mine = members[ci]
     me = mine.index(rank)
     NQ = len(mine)
+    NS = len(STAGES)
     partner = members[1 - ci][me]
     peers = [mine[(me + k) % NQ] for k in range(1, NQ)]
     on_mask = topo.mask(core, T.cores[peers[0]])
@@ -122,21 +127,25 @@ def rank_program(g, core, T, topo):
         sent[lsem] = sent.get(lsem, 0) + ne_on
 
     PB = [T["bank%d" % i] for i in range(8)]
+    eye = T.rep[:, 0:128]
 
     dm = load("y", T.mc[:], T.mu[:], "ldm")
     dxl = load("s", T.dx[:, 64:128], T.x[:], "ldx")
     da = load("y", T.angi[:], T.ang[:], "lda")
     dc = load("y", T.cnt[:], T.counts[:], "ldc")
-    ones = op("v", ms(T.rep[:], 1.0))
-    one2 = op("v", ms(T.eye[:], 1.0))
-    tails = [op("v", ms(T.D[:, 4096:4104], 1.0))]
-    for b in (T.X, T.W, T.f):
-        tails.append(op("v", ms(b[:, 4096:4104], 0.0)))
+    ones = op("v", ms(eye, 1.0))
+    c_eye = op("q", lambda e: e.affine_select(eye, eye, [[-1, 128]], A.is_equal, 0.0, 0, 1), [ones])
     c_p = op("q", lambda e: e.iota(T.ip[:], [[0, 1]], 0, 1))
     c_a = op("q", lambda e: e.iota(T.a64[:], [[2, 64]], -63, 0, allow_small_or_imprecise_dtypes=True))
     c_b = op("q", lambda e: e.iota(T.b4i[:], [[32, 4]], 0, 0, allow_small_or_imprecise_dtypes=True))
     c_z = op("q", lambda e: e.iota(T.ipz[:], [[-1, 16]], 0, 1))
-    c_rep = op("q", lambda e: e.affine_select(T.rep[:], T.rep[:], [[-1, 8], [0, 8], [-8, 16]], A.is_equal, 0.0, 0, 1), [ones])
+    tails = [op("v", ms(T.D[:, 4096:4104], 1.0))]
+    for b in (T.X, T.W, T.f):
+        tails.append(op("v", ms(b[:, 4096:4104], 0.0)))
+    c_rep = [c_eye]
+    for j in range(1, 8):
+        o = T.rep[:, 128 * j:128 * j + 128]
+        c_rep.append(op("v", cp(o, eye), [c_eye]) if j < 5 else op("s", act(o, eye), [c_eye]))
     send(partner, T.pdx[:, 64:128], T.dx[:, 64:128], "cx", [dxl])
 
     sq = [T.sq[:, 64 * i:64 * i + 64] for i in range(3)]
@@ -151,15 +160,17 @@ def rank_program(g, core, T, topo):
     r4 = op("v", tt(sq[0], rq[4], rq[3], A.mult), [r0, r3])
     d_c = op("v", ts(T.dx[:, 0:64], sq[0], 1.0, A.add), [r4])
     send(partner, T.pdx[:, 0:64], T.dx[:, 0:64], "cd", [d_c])
-    c_eye = op("q", lambda e: e.affine_select(T.eye[:], T.eye[:], [[-1, 128]], A.is_equal, 0.0, 0, 1), [one2])
 
-    def spread(src, k, deps):
-        return [[op("p", mm(PB[2 * k + half][:, 64 * h:64 * h + 64], T.rep[:, 128 * (4 * half + h):128 * (4 * half + h) + 128],
-                            src, True, True), [c_rep] + deps, 2 * k + half) for h in range(4)][-1] for half in range(2)]
+    def blk(win, q, h0=0, h1=512):
+        return win[:, 512 * q + h0:512 * q + h1]
 
-    def settle(win, q, k, last):
-        return [op("v", cp(win[:, 512 * q:512 * q + 256], PB[2 * k][:, 0:256]), [last[0]], 2 * k),
-                op("s", act(win[:, 512 * q + 256:512 * q + 512], PB[2 * k + 1][:, 0:256]), [last[1]], 2 * k + 1)]
+    def spread(src, k, deps=()):
+        return [[op("p", mm(PB[2 * k + half][:, 64 * h:64 * h + 64], T.rep[:, 4 * half + h:1024:8], src, True, True),
+                    c_rep + list(deps), 2 * k + half) for h in range(4)][-1] for half in range(2)]
+
+    def settle(win, q, k, m):
+        return [op("v", cp(blk(win, q, 0, 256), PB[2 * k][:, 0:256]), [m[0]], 2 * k),
+                op("s", act(blk(win, q, 256, 512), PB[2 * k + 1][:, 0:256]), [m[1]], 2 * k + 1)]
 
     m_d = spread(T.dx[:, 0:64], 0, [d_c])
     m_x = spread(T.dx[:, 64:128], 1, [dxl])
@@ -172,33 +183,35 @@ def rank_program(g, core, T, topo):
     a5 = op("v", ts(T.kc[:], T.b4[:], T.angf[:, 2:3], A.mult, 16384.0, A.add), [a4, a2])
     a6 = op("v", ts(T.kr[:], T.b4[:], T.angf[:, 0:1], A.mult, 16384.0, A.add), [a4])
     e_d = settle(T.D, rank, 0, m_d)
-    push(T.D[:, 512 * rank:512 * rank + 512], "pd0", "ld0", e_d)
+    push(blk(T.D, rank), "pd0", "ld0", e_d)
     for k in range(4):
         lc = op("v", ts(T.vc[:, k:256:4], T.a64[:], T.angf[:, 0:1], A.mult, T.kc[:, k:k + 1], A.add), [a5, c_a])
         lr = op("v", ts(T.vr[:, k:256:4], T.a64[:], T.angf[:, 1:2], A.mult, T.kr[:, k:k + 1], A.add), [a6, c_a])
     c1 = op("v", ts(T.col[:], T.vc[:], 9, A.logical_shift_right), [lc])
     c2 = op("v", ts(T.row[:], T.vr[:], 3, A.logical_shift_right, 0x1FFFFFC0, A.bitwise_and), [lr])
-    wait("p", "cd", ne_off)
-    m_dp = spread(T.pdx[:, 0:64], 2, [])
-    wait("p", "cx", ne_off)
-    m_xp = spread(T.pdx[:, 64:128], 3, [])
-    e_dp = settle(T.D, partner, 2, m_dp)
-    push(T.D[:, 512 * partner:512 * partner + 512], "pd1", "ld1", e_dp)
-    e_x = settle(T.X, rank, 1, m_x)
-    push(T.X[:, 512 * rank:512 * rank + 512], "pw0", "lw0", e_x)
-    e_xp = settle(T.X, partner, 3, m_xp)
-    push(T.X[:, 512 * partner:512 * partner + 512], "pw1", "lw1", e_xp)
     c3 = op("v", ts(T.pen[:], T.col[:], 64.0, A.is_ge, 4096.0, A.mult), [c1])
     c4 = op("v", tt(T.raw[:], T.col[:], T.row[:], A.add), [c1, c2])
-    c5 = op("v", ts(T.tp[:], T.vr[:], 9, A.arith_shift_right), [lr])
+    wait("p", "cd", ne_off)
+    m_dp = spread(T.pdx[:, 0:64], 2)
+    wait("p", "cx", ne_off)
+    m_xp = spread(T.pdx[:, 64:128], 3)
+    e_dp = settle(T.D, partner, 2, m_dp)
+    push(blk(T.D, partner), "pd1", "ld1", e_dp)
+    e_d += e_dp
+    e_x = settle(T.X, rank, 1, m_x)
+    push(blk(T.X, rank), "pw0", "lw0", e_x)
+    e_xp = settle(T.X, partner, 3, m_xp)
+    push(blk(T.X, partner), "pw1", "lw1", e_xp)
+    ev = e_x + e_xp
     c6 = op("v", tt(T.raw2[:], T.raw[:], T.pen[:], A.add), [c3, c4])
     fl = op("v", ts(T.fl[:], T.raw2[:], 4096.0, A.min), [c6])
+    in0 = op("v", ms(T.ind[:], 0.0))
+    in1 = op("v", ms(T.ind[:, 0:1024:64], 1.0), [in0])
+    c5 = op("v", ts(T.tp[:], T.vr[:], 9, A.arith_shift_right), [lr])
     tl = op("v", ts(T.tl[:], T.tp[:], 0.0, A.max, 63.0, A.min), [c5])
     s_1 = op("v", ts(T.ipz2[:], T.ipz[:], 15, A.bitwise_and), [c_z])
     s_sel = op("v", ts(T.ssel[:], T.ipz[:], 0.0, A.is_equal, 2048.0, A.mult), [c_z])
     s_sum = op("v", ts(T.ssum[:], T.ipz2[:], 0.0, A.is_equal), [s_1])
-    in0 = op("v", ms(T.ind[:], 0.0))
-    in1 = op("v", ms(T.ind[:, 0:1024:64], 1.0), [in0])
 
     Ew = T.e[:, 0:64]
 
@@ -209,18 +222,17 @@ def rank_program(g, core, T, topo):
     for eng in ("s", "v"):
         wait(eng, "pd0", npush)
         wait(eng, "pd1", npush)
-    DCH = [("v", 48, 64), ("s", 0, 16), ("s", 16, 32), ("s", 32, 48)]
-    dg = {}
-    for eng, a, z in DCH:
-        dg[a] = gath(eng, T.f[:, 64 * a:64 * z], T.D[:], T.fl[:, 4 * a:4 * z], [fl] + e_d + e_dp + tails)
+
+    dg = {a: gath(eng, T.f[:, 64 * a:64 * z], T.D[:], T.fl[:, 4 * a:4 * z], [fl] + e_d + tails) for eng, a, z in DCH}
     wsc = []
-    for _, a, z in DCH:
-        wsc.append(op("v", scan(T.W[:, 64 * a:64 * z], T.ind[:], T.f[:, 64 * a:64 * z], A.max, A.mult), [dg[a], in1]))
+    for eng, a, z in DCH:
+        wsc.append(op("v", scan(T.W[:, 64 * a:64 * z], T.ind[:, 0:64 * (z - a)], T.f[:, 64 * a:64 * z], A.max, A.mult),
+                      [dg[a], in1]))
     d0 = op("v", cp(T.d0[:], T.f[:, 0:4096:64]), wsc)
     fz = op("v", ms(T.f[:, 0:4096:64], 0.0), [d0])
 
     def order(k):
-        idx = list(range(len(STAGES)))
+        idx = list(range(NS))
         if k == R - 1:
             idx.sort(key=lambda i: STAGES[i][0] == ci)
         return idx
@@ -234,25 +246,29 @@ def rank_program(g, core, T, topo):
         for n in range(1, NQ):
             at[(i, n)] = room
             room += chunk(i, n)[1]
-    soff = [sum(h - l for _, l, h in STAGES[:i]) // 8 for i in range(len(STAGES))]
+    soff = [sum(h - l for _, l, h in STAGES[:i]) // 8 for i in range(NS)]
+
+    def xgath(eng, a, z):
+        return (a, z, gath(eng, T.xg[:, 64 * a:64 * z], T.X[:], T.fl[:, 4 * a:4 * z], [fl] + ev + tails))
 
     def hscan(a, z, dep):
         lo = 64 * a - 1 if a else None
         return op("v", scan(T.st[:, 64 * z - 1:lo:-1], T.f[:, 64 * z:64 * a:-1], T.xg[:, 64 * z - 1:lo:-1]), [dep, fz])
 
     wbg, loc, run = {}, {}, [0]
-    ev = e_x + e_xp
     for k in range(R):
         last = k == R - 1
         for eng in ("s", "v"):
-            for n in (("pw0", "pw1") if k == 0 else ["pu_%d_%d" % (k - 1, i) for i in range(len(STAGES))]):
+            for n in ["pu_%d_%d" % (k - 1, i) for i in range(NS)] if k else ["pw0", "pw1"]:
                 wait(eng, n, npush)
-
-        def xgath(eng, a, z):
-            return (a, z, gath(eng, T.xg[:, 64 * a:64 * z], T.X[:], T.fl[:, 4 * a:4 * z], ev + tails))
-
         ordr = order(k)
         seq = [(i, n) for i in ordr for n in range(NQ)]
+        for i in ordr:
+            p, w = chunk(i, NQ - 1)
+            nb = w // 128
+            for b in range(nb):
+                mo = op("p", mm(PB[0][:, soff[i] + b:soff[i] + 16 * nb:nb], T.X[:, p + 128 * b:p + 128 * b + 128],
+                                T.ssel[:], True, True), [s_sel] + ev, 0)
         if k == 0:
             sc = [xgath("s", a, a + 16) for a in range(0, 64, 16)]
             done = 0
@@ -268,33 +284,39 @@ def rank_program(g, core, T, topo):
             hs = [hscan(*va), hscan(*sc[0])]
             vb = xgath("v", 8, 14)
             hs += [hscan(*c) for c in [sc[1], vb] + sc[2:]]
+        om = op("s", act(T.old[:], PB[0][:, 0:128]), [mo, hist.get("old")], 0)
         e0 = op("v", tt(T.u[:], T.d0[:], T.st[:, 0:4096:64], A.mult), hs + [d0])
         ee = op("v", tt(T.e[:], T.cnt[:], T.u[:], A.subtract), [e0, dc])
 
-        def place(c):
+        def place(c, eng):
             p, w = chunk(*c)
-            loc[c] = op("s", act(PB[2 + at[c] // 512][:, at[c] % 512:at[c] % 512 + w], T.wb[:, p:p + w]), [wbg[c]],
-                        2 + at[c] // 512)
+            b, o = 2 + at[c] // 512, at[c] % 512
+            o = PB[b][:, o:o + w]
+            loc[c] = op(eng, mm(o, eye, T.wb[:, p:p + w], True, True) if eng == "p" else act(o, T.wb[:, p:p + w]), [wbg[c]], b)
 
-        egd, bsum, part = {}, {}, {}
+        egd, bsum, part, pts = {}, {}, {}, {}
         inp = [c for c in seq if c in at]
         if k == 0:
-            for c in inp[:4]:
-                place(c)
+            for c in inp[:PLP]:
+                place(c, "p")
         for c in inp:
             if c not in loc:
-                place(c)
+                place(c, "s")
             p, w = chunk(*c)
             egd[c] = gath("s", T.eg[:, at[c]:at[c] + w], Ew, T.tl[:, p // 16:(p + w) // 16], [ee, tl])
 
         def evac(n):
             c = seq[n]
-            w = chunk(*c)[1] // 8
+            i, w = c[0], chunk(*c)[1] // 8
             o = T.snd[:, run[0]:run[0] + w]
             run[0] += w
-            part[c] = (o, op("v", cp(o, PB[n % 2][:, 0:w]), [bsum[c]], n % 2))
-
-        pts = {}
+            if c[1] == NQ - 1:
+                d = hist["old"] = op("v", tt(o, PB[n % 2][:, 0:w], T.old[:, soff[i]:soff[i] + w], A.add), [bsum[c], om], n % 2)
+            else:
+                d = op("v", cp(o, PB[n % 2][:, 0:w]), [bsum[c]], n % 2)
+                m = 3 * (128 * k + soff[i]) + c[1] * w
+                send(peers[c[1]], T.lnd[:, m:m + w], o, "rs_%d_%d" % (k, i), [d])
+            part[c] = (o, d)
 
         def chipsum(i):
             w = chunk(i, 0)[1] // 8
@@ -304,49 +326,12 @@ def rank_program(g, core, T, topo):
             o, d = part[(i, NQ - 1)]
             b = op("v", tt(T.t2[:, 0:w], T.lnd[:, 3 * m + 2 * w:3 * m + 3 * w], o, A.add), [d])
             hist["pt"] = pts[i] = op("v", tt(T.pt[:, m:m + w], T.t1[:, 0:w], T.t2[:, 0:w], A.add), [a, b])
-
-        due, todo = {}, list(ordr)
-        for n, c in enumerate(seq):
-            p, w = chunk(*c)
-            out = T.pr[:, p:p + w]
-            if c in at:
-                b, r = 2 + at[c] // 512, at[c] % 512
-                pd = op("v", tt(out, T.eg[:, at[c]:at[c] + w], PB[b][:, r:r + w], A.mult), [egd[c], loc[c]], b)
-            else:
-                pd = op("v", tt(out, Ew.indirect(T.tl[:, p // 16:(p + w) // 16]), T.wb[:, p:p + w], A.mult), [ee, wbg[c], tl])
-            own = c[1] == NQ - 1
-            nb = w // 128
-            for b in range(nb):
-                o = PB[n % 2][:, b:16 * nb:nb]
-                px = slice(p + 128 * b, p + 128 * b + 128)
-                if own:
-                    op("p", mm(o, T.X[:, px], T.ssel[:], True, False), [s_sel] + ev, n % 2)
-                bsum[c] = op("p", mm(o, T.pr[:, px], T.ssum[:], not own, True), [pd, s_sum], n % 2)
-            if n:
-                evac(n - 1)
-            for i in due:
-                due[i] += w
-            if own:
-                due[c[0]] = 0
-            while due.get(todo[0], -1) >= LAG:
-                chipsum(todo.pop(0))
-        evac(len(seq) - 1)
-        for i in todo:
-            chipsum(i)
-        for c in seq:
-            p, w = chunk(*c)
-            if c[1] < NQ - 1:
-                m = 3 * (128 * k + soff[c[0]]) + c[1] * w // 8
-                send(peers[c[1]], T.lnd[:, m:m + w // 8], part[c][0], "rs_%d_%d" % (k, c[0]), [part[c][1]])
-        for i in ordr:
-            m, w = 128 * k + soff[i], chunk(i, 0)[1] // 8
             if not last or STAGES[i][0] != ci:
                 send(partner, T.xs[:, m:m + w], T.pt[:, m:m + w], "xc_%d_%d" % (k, i), [pts[i]])
 
         evs = []
-        for i in ordr:
-            if last and STAGES[i][0] != ci:
-                continue
+
+        def newact(i):
             p, w = chunk(i, NQ - 1)
             nb, w8, m, r, h = w // 128, w // 8, 128 * k + soff[i], 8 * soff[i], w // 2
             wait("v", "xc_%d_%d" % (k, i), ne_off)
@@ -358,10 +343,10 @@ def rank_program(g, core, T, topo):
                     o, f = T.rp[:, r + w8 * j:r + w8 * j + w8], T.rp[:, r:r + w8]
                     cps.append(op("v", cp(o, f), [n]) if j < 4 else op("s", act(o, f), [n]))
                 for eng in ("v", "s"):
-                    for b in (["lp_%d_%d" % (k - 1, i)] if k else ["lw0", "lw1"]):
+                    for b in ["lp_%d_%d" % (k - 1, i)] if k else ["lw0", "lw1"]:
                         wait(eng, b, ne_on)
             hb = nb // 2
-            tp = [op("p", mm(PB[b // hb][0:rows, 128 * (b % hb):128 * (b % hb) + 128], T.rp[:, r + b:r + rows * nb:nb], T.eye[:],
+            tp = [op("p", mm(PB[b // hb][0:rows, 128 * (b % hb):128 * (b % hb) + 128], T.rp[:, r + b:r + rows * nb:nb], eye,
                              True, True), cps + [c_eye], b // hb) for b in range(nb)]
             hist[i] = tp[-1]
             ab = [op("v", ts(win[0:rows, lo:lo + h], PB[0][0:rows, 0:h], STEP, A.mult, 0.0, A.max), [tp[hb - 1]], 0),
@@ -371,7 +356,36 @@ def rank_program(g, core, T, topo):
                 load("y", T.y[:, lo:lo + w], T.ysb[0:16, lo:lo + w], "yo")
             else:
                 push(T.X[:, p:p + w], "pu_%d_%d" % (k, i), "lp_%d_%d" % (k, i), ab)
-                evs += ab
+                evs.extend(ab)
+
+        due, todo = {}, list(ordr)
+        for n, c in enumerate(seq):
+            p, w = chunk(*c)
+            out = T.pr[:, p:p + w]
+            if c in at:
+                b, r = 2 + at[c] // 512, at[c] % 512
+                pd = op("v", tt(out, T.eg[:, at[c]:at[c] + w], PB[b][:, r:r + w], A.mult), [egd[c], loc[c]], b)
+            else:
+                pd = op("v", tt(out, Ew.indirect(T.tl[:, p // 16:(p + w) // 16]), T.wb[:, p:p + w], A.mult), [ee, wbg[c], tl])
+            nb = w // 128
+            for b in range(nb):
+                bsum[c] = op("p", mm(PB[n % 2][:, b:16 * nb:nb], T.pr[:, p + 128 * b:p + 128 * b + 128], T.ssum[:], True, True),
+                             [pd, s_sum], n % 2)
+            if n:
+                evac(n - 1)
+            for i in due:
+                due[i] += w
+            if c[1] == NQ - 1:
+                due[c[0]] = 0
+            while todo and due.get(todo[0], -1) >= LAG:
+                chipsum(todo.pop(0))
+        evac(len(seq) - 1)
+        for what, j in TAIL:
+            i = ordr[j]
+            if what == "c" and i in todo:
+                chipsum(i)
+            if what == "n" and (not last or STAGES[i][0] == ci):
+                newact(i)
         ev = evs
 
     for e in ("v", "s", "p", "q"):

from concourse.bass import DstId, RemoteDMATransfer
from concourse.mybir import AluOpType as A, ActivationFunctionType as AF

R = 3
STEP = 2.0 ** -12
STAGES = [(0, 0, 512), (1, 0, 512)]
LAG = 1536
WBV = 5
PLP = 3
DCH = [("v", 52, 64), ("s", 0, 14), ("s", 14, 28), ("s", 28, 42), ("s", 42, 52)]
TAIL = [("c", 0), ("c", 1), ("n", 0), ("n", 1)]
KQ = 0.00012918686694904754
QUAD = [(1.1219518404595346, 18.754011438386996), (-4.267052247540635, 2.746736091488364),
        (-1.8906565018022652, 14.883958171039492)]
SCRATCH = {}
for _n, _w in (("mc", 64), ("dx", 128), ("pdx", 128), ("angf", 4), ("cnt", 64), ("sq", 192), ("rq", 320),
               ("rep", 1024), ("ssum", 16), ("ssel", 16), ("fm", 1), ("a64", 64), ("b4i", 4), ("b4", 4), ("kc", 4),
               ("kr", 4), ("pen", 256), ("raw", 256), ("raw2", 256), ("D", 4104), ("X", 4104), ("W", 4104), ("f", 4104),
               ("ind", 1024), ("xg", 4096), ("st", 4096), ("wb", 4096), ("pr", 4096), ("eg", 3072), ("u", 64), ("e", 64),
               ("snd", 1536), ("lnd", 1152), ("t1", 64), ("t2", 64), ("pt", 384), ("xs", 384), ("rp", 1024), ("ysb", 512),
               ("d0", 64), ("old", 128)):
    SCRATCH[_n] = ("sbuf", [128, _w], "float32")
for _n, _w in (("angi", 2), ("ipz", 16), ("ipz2", 16), ("ip", 1), ("ip2", 1), ("vc", 256), ("vr", 256), ("col", 256),
               ("row", 256), ("tp", 256)):
    SCRATCH[_n] = ("sbuf", [128, _w], "int32")
for _n in ("fl", "tl"):
    SCRATCH[_n] = ("sbuf", [128, 256], "uint16")
for _n in range(8):
    SCRATCH["bank%d" % _n] = ("psum", [128, 512], "float32")
SEMAPHORES = (["v", "s", "p", "q", "ldm", "ldx", "lda", "ldc", "yo", "cx", "cd", "lr"]
              + ["pd0", "pd1", "pw0", "pw1", "ld0", "ld1", "lw0", "lw1"]
              + ["%s_%d_%d" % (n, k, s) for n in ("rs", "xc", "pu", "lp") for k in range(R) for s in range(len(STAGES))])


def ts(out, i, s1, o0, s2=None, o1=None):
    if o1 is None:
        return lambda e: e.tensor_scalar(out, i, s1, None, o0)
    return lambda e: e.tensor_scalar(out, i, s1, s2, o0, o1)


def tt(out, a, b, o):
    return lambda e: e.tensor_tensor(out, a, b, o)


def cp(out, i):
    return lambda e: e.tensor_copy(out, i)


def act(out, i, fn=AF.Copy, scale=1.0):
    return lambda e: e.activation(out, i, fn, scale=scale)


def mm(out, l, r, a, z):
    return lambda e: e.matmul(out, l, r, a, z)


def ms(ap, c):
    return lambda e: e.memset(ap, c)


def scan(out, d0, d1, o0=A.mult, o1=A.add):
    return lambda e: e.tensor_tensor_scan(out, d0, d1, 0.0, o0, o1)


def rank_program(g, core, T, topo):
    rank = T.rank_of(core)
    if rank is None:
        return
    chips = []
    for c in T.cores:
        if topo.chip(c) not in chips:
            chips.append(topo.chip(c))
    members = [[r for r, c in enumerate(T.cores) if topo.chip(c) == ch] for ch in chips]
    ci = chips.index(topo.chip(core))
    mine = members[ci]
    me = mine.index(rank)
    NQ = len(mine)
    NS = len(STAGES)
    partner = members[1 - ci][me]
    peers = [mine[(me + k) % NQ] for k in range(1, NQ)]
    on_mask = topo.mask(core, T.cores[peers[0]])
    ne_on = len(topo.engines(core, T.cores[peers[0]]))
    ne_off = len(topo.engines(core, T.cores[partner]))
    npush = ne_on * (NQ - 1)

    ENG = {"v": g.vector, "s": g.scalar, "p": g.tensor, "q": g, "y": g.sync}
    cnt, known, touch, sent, hist = {}, {}, {}, {}, {}

    def wait(eng, sem, val):
        if known.get((eng, sem), 0) < val:
            ENG[eng].wait_ge(T.sem[sem], val)
            known[(eng, sem)] = val

    def waits(eng, deps):
        for d in deps:
            if d is not None:
                wait(eng, d[0], d[1])

    def op(eng, fn, deps=(), bank=None):
        waits(eng, deps)
        use = touch.setdefault(bank, {}) if bank is not None else {}
        for (o, n) in use.items():
            if o != eng:
                wait(eng, o, n)
        fn(ENG[eng]).then_inc(T.sem[eng], 1)
        cnt[eng] = cnt.get(eng, 0) + 1
        use[eng] = cnt[eng]
        return (eng, cnt[eng])

    def load(eng, out, in_, sem):
        ENG[eng].dma_start(out, in_).then_inc(T.sem[sem], 16)
        hist[sem] = hist.get(sem, 0) + 16
        return (sem, hist[sem])

    def send(dst, out, in_, rsem, deps):
        waits("q", deps)
        c = T.cores[dst]
        rid, pid, _ = topo.addr(c)
        g.remote_dma(out, in_, T.sem[rsem], T.sem.lr, pid, rid, topo.mask(core, c))
        sent["lr"] = sent.get("lr", 0) + len(topo.engines(core, c))

    def push(ap, rsem, lsem, deps):
        waits("q", deps)
        ids = [DstId(rid=topo.addr(T.cores[r])[0], pnc=topo.addr(T.cores[r])[1]) for r in peers]
        g.remote_dma_fused([RemoteDMATransfer(dst_ids=ids, dma_engine_mask=on_mask, remote_sem=T.sem[rsem], srcs=[ap],
                                              dsts=[ap] * len(peers), alu_op=0)], local_sem=T.sem[lsem])
        sent[lsem] = sent.get(lsem, 0) + ne_on

    PB = [T["bank%d" % i] for i in range(8)]
    eye = T.rep[:, 0:128]

    dm = load("y", T.mc[:], T.mu[:], "ldm")
    dxl = load("s", T.dx[:, 64:128], T.x[:], "ldx")
    da = load("y", T.angi[:], T.ang[:], "lda")
    dc = load("y", T.cnt[:], T.counts[:], "ldc")
    ones = op("v", ms(eye, 1.0))
    c_eye = op("q", lambda e: e.affine_select(eye, eye, [[-1, 128]], A.is_equal, 0.0, 0, 1), [ones])
    c_p = op("q", lambda e: e.iota(T.ip[:], [[0, 1]], 0, 1))
    c_a = op("q", lambda e: e.iota(T.a64[:], [[2, 64]], -63, 0, allow_small_or_imprecise_dtypes=True))
    c_b = op("q", lambda e: e.iota(T.b4i[:], [[32, 4]], 0, 0, allow_small_or_imprecise_dtypes=True))
    c_z = op("q", lambda e: e.iota(T.ipz[:], [[-1, 16]], 0, 1))
    tails = [op("v", ms(T.D[:, 4096:4104], 1.0))]
    for b in (T.X, T.W, T.f):
        tails.append(op("v", ms(b[:, 4096:4104], 0.0)))
    c_rep = [c_eye]
    for j in range(1, 8):
        o = T.rep[:, 128 * j:128 * j + 128]
        c_rep.append(op("v", cp(o, eye), [c_eye]) if j < 5 else op("s", act(o, eye), [c_eye]))
    send(partner, T.pdx[:, 64:128], T.dx[:, 64:128], "cx", [dxl])

    sq = [T.sq[:, 64 * i:64 * i + 64] for i in range(3)]
    rq = [T.rq[:, 64 * i:64 * i + 64] for i in range(5)]
    sb = [op("v", ts(sq[i], T.mc[:], QUAD[i][0], A.add), [dm]) for i in range(3)]
    ss = [op("s", act(sq[i], sq[i], AF.Square), [sb[i]]) for i in range(3)]
    r0 = op("v", ts(rq[0], sq[0], QUAD[0][1], A.add, -KQ, A.mult), [ss[0]])
    r1 = op("v", ts(rq[1], sq[1], QUAD[1][1], A.add), [ss[1]])
    r2 = op("v", ts(rq[2], sq[2], QUAD[2][1], A.add), [ss[2]])
    r0 = op("v", tt(rq[3], rq[0], T.mc[:], A.mult), [r0])
    r3 = op("v", tt(rq[4], rq[1], rq[2], A.mult), [r1, r2])
    r4 = op("v", tt(sq[0], rq[4], rq[3], A.mult), [r0, r3])
    d_c = op("v", ts(T.dx[:, 0:64], sq[0], 1.0, A.add), [r4])
    send(partner, T.pdx[:, 0:64], T.dx[:, 0:64], "cd", [d_c])

    def blk(win, q, h0=0, h1=512):
        return win[:, 512 * q + h0:512 * q + h1]

    def spread(src, k, deps=()):
        return [[op("p", mm(PB[2 * k + half][:, 64 * h:64 * h + 64], T.rep[:, 4 * half + h:1024:8], src, True, True),
                    c_rep + list(deps), 2 * k + half) for h in range(4)][-1] for half in range(2)]

    def settle(win, q, k, m):
        return [op("v", cp(blk(win, q, 0, 256), PB[2 * k][:, 0:256]), [m[0]], 2 * k),
                op("s", act(blk(win, q, 256, 512), PB[2 * k + 1][:, 0:256]), [m[1]], 2 * k + 1)]

    m_d = spread(T.dx[:, 0:64], 0, [d_c])
    m_x = spread(T.dx[:, 64:128], 1, [dxl])

    a0 = op("v", cp(T.angf[:, 0:2], T.angi[:]), [da])
    a1 = op("v", ts(T.ip2[:], T.ip[:], 15, A.bitwise_and), [c_p])
    a2 = op("v", ts(T.angf[:, 2:3], T.angf[:, 1:2], -1.0, A.mult), [a0])
    a3 = op("v", ts(T.fm[:], T.ip2[:], 2.0, A.mult, -63.0, A.add), [a1])
    a4 = op("v", ts(T.b4[:], T.b4i[:], T.fm[:, 0:1], A.add), [a3, c_b])
    a5 = op("v", ts(T.kc[:], T.b4[:], T.angf[:, 2:3], A.mult, 16384.0, A.add), [a4, a2])
    a6 = op("v", ts(T.kr[:], T.b4[:], T.angf[:, 0:1], A.mult, 16384.0, A.add), [a4])
    e_d = settle(T.D, rank, 0, m_d)
    push(blk(T.D, rank), "pd0", "ld0", e_d)
    for k in range(4):
        lc = op("v", ts(T.vc[:, k:256:4], T.a64[:], T.angf[:, 0:1], A.mult, T.kc[:, k:k + 1], A.add), [a5, c_a])
        lr = op("v", ts(T.vr[:, k:256:4], T.a64[:], T.angf[:, 1:2], A.mult, T.kr[:, k:k + 1], A.add), [a6, c_a])
    c1 = op("v", ts(T.col[:], T.vc[:], 9, A.logical_shift_right), [lc])
    c2 = op("v", ts(T.row[:], T.vr[:], 3, A.logical_shift_right, 0x1FFFFFC0, A.bitwise_and), [lr])
    c3 = op("v", ts(T.pen[:], T.col[:], 64.0, A.is_ge, 4096.0, A.mult), [c1])
    c4 = op("v", tt(T.raw[:], T.col[:], T.row[:], A.add), [c1, c2])
    wait("p", "cd", ne_off)
    m_dp = spread(T.pdx[:, 0:64], 2)
    wait("p", "cx", ne_off)
    m_xp = spread(T.pdx[:, 64:128], 3)
    e_dp = settle(T.D, partner, 2, m_dp)
    push(blk(T.D, partner), "pd1", "ld1", e_dp)
    e_d += e_dp
    e_x = settle(T.X, rank, 1, m_x)
    push(blk(T.X, rank), "pw0", "lw0", e_x)
    e_xp = settle(T.X, partner, 3, m_xp)
    push(blk(T.X, partner), "pw1", "lw1", e_xp)
    ev = e_x + e_xp
    c6 = op("v", tt(T.raw2[:], T.raw[:], T.pen[:], A.add), [c3, c4])
    fl = op("v", ts(T.fl[:], T.raw2[:], 4096.0, A.min), [c6])
    in0 = op("v", ms(T.ind[:], 0.0))
    in1 = op("v", ms(T.ind[:, 0:1024:64], 1.0), [in0])
    c5 = op("v", ts(T.tp[:], T.vr[:], 9, A.arith_shift_right), [lr])
    tl = op("v", ts(T.tl[:], T.tp[:], 0.0, A.max, 63.0, A.min), [c5])
    s_1 = op("v", ts(T.ipz2[:], T.ipz[:], 15, A.bitwise_and), [c_z])
    s_sel = op("v", ts(T.ssel[:], T.ipz[:], 0.0, A.is_equal, 2048.0, A.mult), [c_z])
    s_sum = op("v", ts(T.ssum[:], T.ipz2[:], 0.0, A.is_equal), [s_1])

    Ew = T.e[:, 0:64]

    def gath(eng, out, win, off, deps):
        src = win.indirect(off)
        return op(eng, cp(out, src) if eng == "v" else act(out, src), deps)

    for eng in ("s", "v"):
        wait(eng, "pd0", npush)
        wait(eng, "pd1", npush)

    dg = {a: gath(eng, T.f[:, 64 * a:64 * z], T.D[:], T.fl[:, 4 * a:4 * z], [fl] + e_d + tails) for eng, a, z in DCH}
    wsc = []
    for eng, a, z in DCH:
        wsc.append(op("v", scan(T.W[:, 64 * a:64 * z], T.ind[:, 0:64 * (z - a)], T.f[:, 64 * a:64 * z], A.max, A.mult),
                      [dg[a], in1]))
    d0 = op("v", cp(T.d0[:], T.f[:, 0:4096:64]), wsc)
    fz = op("v", ms(T.f[:, 0:4096:64], 0.0), [d0])

    def order(k):
        idx = list(range(NS))
        if k == R - 1:
            idx.sort(key=lambda i: STAGES[i][0] == ci)
        return idx

    def chunk(i, n):
        s, lo, hi = STAGES[i]
        return 512 * members[s][(me + 1 + n) % NQ] + lo, hi - lo

    at, room = {}, 0
    for i in order(0):
        for n in range(1, NQ):
            at[(i, n)] = room
            room += chunk(i, n)[1]
    soff = [sum(h - l for _, l, h in STAGES[:i]) // 8 for i in range(NS)]

    def xgath(eng, a, z):
        return (a, z, gath(eng, T.xg[:, 64 * a:64 * z], T.X[:], T.fl[:, 4 * a:4 * z], [fl] + ev + tails))

    def hscan(a, z, dep):
        lo = 64 * a - 1 if a else None
        return op("v", scan(T.st[:, 64 * z - 1:lo:-1], T.f[:, 64 * z:64 * a:-1], T.xg[:, 64 * z - 1:lo:-1]), [dep, fz])

    wbg, loc, run = {}, {}, [0]
    for k in range(R):
        last = k == R - 1
        for eng in ("s", "v"):
            for n in ["pu_%d_%d" % (k - 1, i) for i in range(NS)] if k else ["pw0", "pw1"]:
                wait(eng, n, npush)
        ordr = order(k)
        seq = [(i, n) for i in ordr for n in range(NQ)]
        for i in ordr:
            p, w = chunk(i, NQ - 1)
            nb = w // 128
            for b in range(nb):
                mo = op("p", mm(PB[0][:, soff[i] + b:soff[i] + 16 * nb:nb], T.X[:, p + 128 * b:p + 128 * b + 128],
                                T.ssel[:], True, True), [s_sel] + ev, 0)
        if k == 0:
            sc = [xgath("s", a, a + 16) for a in range(0, 64, 16)]
            done = 0
            for c in seq:
                p, w = chunk(*c)
                wbg[c] = gath("v" if done < 512 * WBV else "s", T.wb[:, p:p + w], T.W[:], T.fl[:, p // 16:(p + w) // 16],
                              wsc + tails)
                done += w
            hs = [hscan(*c) for c in sc]
        else:
            sc = [xgath("s", a, z) for a, z in ((14, 26), (26, 38), (38, 50), (50, 60), (60, 64))]
            va = xgath("v", 0, 8)
            hs = [hscan(*va), hscan(*sc[0])]
            vb = xgath("v", 8, 14)
            hs += [hscan(*c) for c in [sc[1], vb] + sc[2:]]
        om = op("s", act(T.old[:], PB[0][:, 0:128]), [mo, hist.get("old")], 0)
        e0 = op("v", tt(T.u[:], T.d0[:], T.st[:, 0:4096:64], A.mult), hs + [d0])
        ee = op("v", tt(T.e[:], T.cnt[:], T.u[:], A.subtract), [e0, dc])

        def place(c, eng):
            p, w = chunk(*c)
            b, o = 2 + at[c] // 512, at[c] % 512
            o = PB[b][:, o:o + w]
            loc[c] = op(eng, mm(o, eye, T.wb[:, p:p + w], True, True) if eng == "p" else act(o, T.wb[:, p:p + w]), [wbg[c]], b)

        egd, bsum, part, pts = {}, {}, {}, {}
        inp = [c for c in seq if c in at]
        if k == 0:
            for c in inp[:PLP]:
                place(c, "p")
        for c in inp:
            if c not in loc:
                place(c, "s")
            p, w = chunk(*c)
            egd[c] = gath("s", T.eg[:, at[c]:at[c] + w], Ew, T.tl[:, p // 16:(p + w) // 16], [ee, tl])

        def evac(n):
            c = seq[n]
            i, w = c[0], chunk(*c)[1] // 8
            o = T.snd[:, run[0]:run[0] + w]
            run[0] += w
            if c[1] == NQ - 1:
                d = hist["old"] = op("v", tt(o, PB[n % 2][:, 0:w], T.old[:, soff[i]:soff[i] + w], A.add), [bsum[c], om], n % 2)
            else:
                d = op("v", cp(o, PB[n % 2][:, 0:w]), [bsum[c]], n % 2)
                m = 3 * (128 * k + soff[i]) + c[1] * w
                send(peers[c[1]], T.lnd[:, m:m + w], o, "rs_%d_%d" % (k, i), [d])
            part[c] = (o, d)

        def chipsum(i):
            w = chunk(i, 0)[1] // 8
            m = 128 * k + soff[i]
            wait("v", "rs_%d_%d" % (k, i), npush)
            a = op("v", tt(T.t1[:, 0:w], T.lnd[:, 3 * m:3 * m + w], T.lnd[:, 3 * m + w:3 * m + 2 * w], A.add), [hist.get("pt")])
            o, d = part[(i, NQ - 1)]
            b = op("v", tt(T.t2[:, 0:w], T.lnd[:, 3 * m + 2 * w:3 * m + 3 * w], o, A.add), [d])
            hist["pt"] = pts[i] = op("v", tt(T.pt[:, m:m + w], T.t1[:, 0:w], T.t2[:, 0:w], A.add), [a, b])
            if not last or STAGES[i][0] != ci:
                send(partner, T.xs[:, m:m + w], T.pt[:, m:m + w], "xc_%d_%d" % (k, i), [pts[i]])

        evs = []

        def newact(i):
            p, w = chunk(i, NQ - 1)
            nb, w8, m, r, h = w // 128, w // 8, 128 * k + soff[i], 8 * soff[i], w // 2
            wait("v", "xc_%d_%d" % (k, i), ne_off)
            n = op("v", tt(T.rp[:, r:r + w8], T.pt[:, m:m + w8], T.xs[:, m:m + w8], A.add), [pts[i], hist.get(i)])
            cps, rows, win, lo = [n], 16, T.ysb, p % 512
            if not last:
                rows, win, lo = 128, T.X, p
                for j in range(1, 8):
                    o, f = T.rp[:, r + w8 * j:r + w8 * j + w8], T.rp[:, r:r + w8]
                    cps.append(op("v", cp(o, f), [n]) if j < 4 else op("s", act(o, f), [n]))
                for eng in ("v", "s"):
                    for b in ["lp_%d_%d" % (k - 1, i)] if k else ["lw0", "lw1"]:
                        wait(eng, b, ne_on)
            hb = nb // 2
            tp = [op("p", mm(PB[b // hb][0:rows, 128 * (b % hb):128 * (b % hb) + 128], T.rp[:, r + b:r + rows * nb:nb], eye,
                             True, True), cps + [c_eye], b // hb) for b in range(nb)]
            hist[i] = tp[-1]
            ab = [op("v", ts(win[0:rows, lo:lo + h], PB[0][0:rows, 0:h], STEP, A.mult, 0.0, A.max), [tp[hb - 1]], 0),
                  op("s", act(win[0:rows, lo + h:lo + w], PB[1][0:rows, 0:h], AF.Relu, STEP), [tp[-1]], 1)]
            if last:
                waits("y", ab)
                load("y", T.y[:, lo:lo + w], T.ysb[0:16, lo:lo + w], "yo")
            else:
                push(T.X[:, p:p + w], "pu_%d_%d" % (k, i), "lp_%d_%d" % (k, i), ab)
                evs.extend(ab)

        due, todo = {}, list(ordr)
        for n, c in enumerate(seq):
            p, w = chunk(*c)
            out = T.pr[:, p:p + w]
            if c in at:
                b, r = 2 + at[c] // 512, at[c] % 512
                pd = op("v", tt(out, T.eg[:, at[c]:at[c] + w], PB[b][:, r:r + w], A.mult), [egd[c], loc[c]], b)
            else:
                pd = op("v", tt(out, Ew.indirect(T.tl[:, p // 16:(p + w) // 16]), T.wb[:, p:p + w], A.mult), [ee, wbg[c], tl])
            nb = w // 128
            for b in range(nb):
                bsum[c] = op("p", mm(PB[n % 2][:, b:16 * nb:nb], T.pr[:, p + 128 * b:p + 128 * b + 128], T.ssum[:], True, True),
                             [pd, s_sum], n % 2)
            if n:
                evac(n - 1)
            for i in due:
                due[i] += w
            if c[1] == NQ - 1:
                due[c[0]] = 0
            while todo and due.get(todo[0], -1) >= LAG:
                chipsum(todo.pop(0))
        evac(len(seq) - 1)
        for what, j in TAIL:
            i = ordr[j]
            if what == "c" and i in todo:
                chipsum(i)
            if what == "n" and (not last or STAGES[i][0] == ci):
                newact(i)
        ev = evs

    for e in ("v", "s", "p", "q"):
        wait("q", e, cnt[e])
    for n in sorted(sent):
        wait("q", n, sent[n])
    for n in ("ldm", "ldx", "lda", "ldc", "yo"):
        wait("q", n, hist[n])
